import numpy as np
import ml_dtypes

BF16 = ml_dtypes.bfloat16


def bf(x):
    return np.asarray(x, np.float32).astype(BF16)


def f32(x):
    return np.asarray(x, np.float32)


def f64(x):
    return np.asarray(x).astype(np.float64)


def striped(idx):
    return np.tile(idx.reshape(-1, 16).T, (8, 1))


S, K, M, N, V, F = 512, 128, 128, 1024, 128, 8


def setup_inputs():
    return {"table": bf(np.random.standard_normal((F, K, S))), "w": bf(np.random.standard_normal((F, K, M)) / np.sqrt(F * K)), "b": f32(0.5 * np.random.standard_normal((M, 1))), "offs": striped(np.concatenate([np.random.permutation(np.tile(np.arange(S), 2))[:V] for _ in range(F)]))}


def reference(table, w, b, offs):
    idx = offs[:16].T.reshape(-1)
    y = sum(f64(w)[f].T @ f64(table)[f][:, idx[f * V : (f + 1) * V]] for f in range(F))
    return y + f64(b)

@@ -1,0 +1,34 @@
+import concourse.mybir as mybir
+
+F, K, S, M, V = 8, 128, 512, 128, 128
+FLOPS = 2 * F * K * M * V
+BF16, F32, U16 = mybir.dt.bfloat16, mybir.dt.float32, mybir.dt.uint16
+LIST_COLS = V // 16
+
+
+def tile_rows_fields_bias_rep_kernel(tc, table, w, b, offs, out):
+    nc = tc.nc
+    with (
+        tc.tile_pool(name="held", bufs=1) as held,
+        tc.psum_pool(name="psum", bufs=1) as psum,
+    ):
+        offsets = held.tile([128, F * LIST_COLS], U16, name="offsets")
+        weights = held.tile([K, F, M], BF16, name="weights")
+        bias = held.tile([M, 1], F32, name="bias")
+        pairs = [held.tile([K, 2, S], BF16, name=f"pair{i}") for i in range(F // 2)]
+
+        nc.sync.dma_start(offsets[:], offs)
+        nc.sync.dma_start(weights[:], w.rearrange("f k m -> k f m"))
+        for i, pair in enumerate(pairs):
+            nc.sync.dma_start(pair[:], table[2 * i : 2 * i + 2].rearrange("f k s -> k f s"))
+        nc.scalar.dma_start(bias[:], b)
+
+        total = psum.tile([M, V], F32, name="total")
+        for f in range(F):
+            window = pairs[f // 2][:, f % 2, :]
+            picked = window.indirect(offsets[:, f * LIST_COLS : (f + 1) * LIST_COLS])
+            nc.tensor.matmul(total[:], weights[:, f, :], picked, start=(f == 0), stop=(f == F - 1))
+
+        result = held.tile([M, V], F32, name="result")
+        nc.vector.tensor_scalar_add(result[:], total[:], bias[:, 0:1])
+        nc.sync.dma_start(out, result[:])

@@ -17,11 +17,12 @@ def tile_rows_fields_bias_rep_kernel(tc, table, w, b, offs, out):
         bias = held.tile([M, 1], F32, name="bias")
         pairs = [held.tile([K, 2, S], BF16, name=f"pair{i}") for i in range(F // 2)]
 
-        nc.sync.dma_start(offsets[:], offs)
-        nc.sync.dma_start(weights[:], w.rearrange("f k m -> k f m"))
+        nc.scalar.dma_start(weights[:], w.rearrange("f k m -> k f m"))
+        nc.scalar.dma_start(bias[:], b)
         for i, pair in enumerate(pairs):
             nc.sync.dma_start(pair[:], table[2 * i : 2 * i + 2].rearrange("f k s -> k f s"))
-        nc.scalar.dma_start(bias[:], b)
+            if i == 0:
+                nc.sync.dma_start(offsets[:], offs)
 
         total = psum.tile([M, V], F32, name="total")
         for f in range(F):

@@ -18,11 +18,11 @@ def tile_rows_fields_bias_rep_kernel(tc, table, w, b, offs, out):
         pairs = [held.tile([K, 2, S], BF16, name=f"pair{i}") for i in range(F // 2)]
 
         nc.scalar.dma_start(weights[:], w.rearrange("f k m -> k f m"))
-        nc.scalar.dma_start(bias[:], b)
         for i, pair in enumerate(pairs):
             nc.sync.dma_start(pair[:], table[2 * i : 2 * i + 2].rearrange("f k s -> k f s"))
             if i == 0:
                 nc.sync.dma_start(offsets[:], offs)
+        nc.sync.dma_start(bias[:], b)
 
         total = psum.tile([M, V], F32, name="total")
         for f in range(F):

import concourse.mybir as mybir

F, K, S, M, V = 8, 128, 512, 128, 128
FLOPS = 2 * F * K * M * V
BF16, F32, U16 = mybir.dt.bfloat16, mybir.dt.float32, mybir.dt.uint16
LIST_COLS = V // 16


def tile_rows_fields_bias_rep_kernel(tc, table, w, b, offs, out):
    nc = tc.nc
    with (
        tc.tile_pool(name="held", bufs=1) as held,
        tc.psum_pool(name="psum", bufs=1) as psum,
    ):
        offsets = held.tile([128, F * LIST_COLS], U16, name="offsets")
        weights = held.tile([K, F, M], BF16, name="weights")
        bias = held.tile([M, 1], F32, name="bias")
        pairs = [held.tile([K, 2, S], BF16, name=f"pair{i}") for i in range(F // 2)]

        nc.scalar.dma_start(weights[:], w.rearrange("f k m -> k f m"))
        for i, pair in enumerate(pairs):
            nc.sync.dma_start(pair[:], table[2 * i : 2 * i + 2].rearrange("f k s -> k f s"))
            if i == 0:
                nc.sync.dma_start(offsets[:], offs)
        nc.sync.dma_start(bias[:], b)

        total = psum.tile([M, V], F32, name="total")
        for f in range(F):
            window = pairs[f // 2][:, f % 2, :]
            picked = window.indirect(offsets[:, f * LIST_COLS : (f + 1) * LIST_COLS])
            nc.tensor.matmul(total[:], weights[:, f, :], picked, start=(f == 0), stop=(f == F - 1))

        result = held.tile([M, V], F32, name="result")
        nc.vector.tensor_scalar_add(result[:], total[:], bias[:, 0:1])
        nc.sync.dma_start(out, result[:])
